import numpy as np
import ml_dtypes


def mxq(x, axis, fmt="e4m3"):
    dtype, down = {"e4m3": (ml_dtypes.float8_e4m3fn, 7), "e5m2": (ml_dtypes.float8_e5m2, 14)}[fmt]
    v = np.moveaxis(np.asarray(x, np.float32).astype(ml_dtypes.bfloat16).astype(np.float64), axis, -1)
    blocks = v.reshape(v.shape[:-1] + (-1, 32))
    amax = np.abs(blocks).max(-1, keepdims=True)
    byte = np.maximum(np.where(amax > 0, np.frexp(amax)[1] - 1 + 127, 0) - down, 1)
    scale = np.exp2(byte - 127.0)
    codes = (blocks / scale).astype(np.float32).astype(dtype).astype(np.float64)
    return np.moveaxis((codes * scale).reshape(v.shape), -1, axis)


WIDE = False


def mx_kscale(k):
    if not WIDE:
        return np.ones(k)
    levels = np.array([10, -10, 5, -5, 0])
    if k % 512:
        return np.exp2(np.random.permutation(np.resize(levels, k // 32))).repeat(32)
    a = np.empty((k // 512, 16))
    for p in range(k // 512):
        a[p, :8] = np.random.permutation(np.resize(levels, 8))
        for g in range(8):
            far = levels[np.abs(levels - a[p, g]) >= 10]
            a[p, g + 8] = far[np.random.randint(len(far))]
    return np.exp2(a.ravel()).repeat(32)


def f64(x):
    return np.asarray(x).astype(np.float64)


def striped(idx):
    return np.tile(idx.reshape(-1, 16).T, (8, 1)).astype(np.uint16)


def unstriped(offs):
    return offs[:16].T.reshape(-1).astype(np.int64)


E2M1 = np.array([0.0, 0.5, 1.0, 1.5, 2.0, 3.0, 4.0, 6.0, -0.0, -0.5, -1.0, -1.5, -2.0, -3.0, -4.0, -6.0])


def pack_weight(w, fmt):
    k, n = w.shape
    w = f64(np.asarray(w, np.float32).astype(ml_dtypes.bfloat16)).reshape(k // 32, 32, n)
    amax = np.abs(w).max(1)
    if fmt == "e4m3":
        byte = np.frexp(amax)[1] - 1 + 127 - 7
    else:
        mant, ex = np.frexp(amax / 6.0)
        byte = np.where(mant > 0.5, ex, ex - 1) + 127
    byte = np.clip(np.where(amax > 0, byte, 1), 1, 254)
    scaled = (w * np.exp2(127.0 - byte)[:, None, :]).reshape(k, n).astype(np.float32)
    by_word = np.ascontiguousarray(scaled.reshape(k // 512, 128, 4, n).transpose(0, 1, 3, 2))
    if fmt == "e4m3":
        words = by_word.astype(ml_dtypes.float8_e4m3fn).view(np.uint8)
    else:
        c = by_word.astype(ml_dtypes.float4_e2m1fn).view(np.uint8) & 0xF
        words = (c[..., 0::2] | (c[..., 1::2] << 4)).reshape(k // 512, 128, 2 * n)
    return np.ascontiguousarray(words), np.ascontiguousarray(byte.astype(np.uint8).reshape(k // 512, 16, n))


def unpack_weight(words, scales, fmt):
    g, _, n = scales.shape
    words = np.ascontiguousarray(words).reshape(g, 128, n, -1)
    if fmt == "e4m3":
        vals = words.view(ml_dtypes.float8_e4m3fn).astype(np.float64)
    else:
        nib = np.empty((g, 128, n, 4), np.uint8)
        nib[..., 0::2] = words & 0xF
        nib[..., 1::2] = words >> 4
        vals = E2M1[nib]
    vals = vals * np.repeat(np.exp2(scales.astype(np.float64) - 127.0), 8, axis=1)[..., None]
    return vals.transpose(0, 1, 3, 2).reshape(g * 512, n)


def gelu(v):
    return 0.5 * v * (1.0 + np.tanh(np.sqrt(2.0 / np.pi) * (v + 0.044715 * v**3)))


K, T, S, H, P, N = 1024, 4096, 1024, 512, 512, 768


def setup_inputs():
    n = np.random.standard_normal
    s = mx_kscale(K)[:, None]
    u = mx_kscale(H)[:, None]
    tab_words, tab_scales = pack_weight(n((K, T)) * s, "e4m3")
    w2_words, w2_scales = pack_weight(0.52 * n((K, H)) / np.sqrt(K) / s, "e2m1")
    wb_words, wb_scales = pack_weight(n((H, N)) / np.sqrt(H) / u, "e4m3")
    return {
        "tab_words": tab_words, "tab_scales": tab_scales,
        "offs": striped(np.random.permutation(T)[:S]),
        "pos1": striped(np.random.permutation(S)[:P]),
        "pos2": striped(np.random.permutation(S)[:P]),
        "w1": (n((K, H)) / np.sqrt(K) / s).astype(np.float32),
        "w2_words": w2_words, "w2_scales": w2_scales,
        "rest": (0.7 * n((H, S))).astype(np.float32),
        "gain": (np.exp(0.3 * n(H)) * u[:, 0]).astype(np.float32),
        "low": (0.6 * n(H) * u[:, 0]).astype(np.float32),
        "wa": (n((H, N)) / np.sqrt(H) / u).astype(np.float32),
        "wb_words": wb_words, "wb_scales": wb_scales,
        "read": np.exp(0.5 * n((N, P))).astype(np.float32),
    }


def reference(tab_words, tab_scales, offs, pos1, pos2, w1, w2_words, w2_scales, rest, gain, low, wa, wb_words, wb_scales, read):
    v = unpack_weight(tab_words, tab_scales, "e4m3")[:, unstriped(offs)]
    w2 = unpack_weight(w2_words, w2_scales, "e2m1")
    wb = unpack_weight(wb_words, wb_scales, "e4m3")
    shape = (mxq(f64(w1), 0, "e4m3").T @ v) + f64(rest)
    phase = w2.T @ v
    h = shape * np.cos(phase) * f64(gain)[:, None]
    xa = np.abs(h[:, unstriped(pos1)])
    xb = np.maximum(h[:, unstriped(pos2)], f64(low)[:, None])
    y = mxq(f64(wa), 0, "e4m3").T @ mxq(xa, 0, "e4m3") + wb.T @ mxq(xb, 0, "e4m3")
    return y * f64(read)

@@ -1,0 +1,249 @@
+import math
+from contextlib import ExitStack
+
+import concourse.mybir as mybir
+
+K, T, S, H, PAIRS, N = 1024, 4096, 1024, 512, 512, 768
+FLOPS = 2 * (2 * K * H * S + 2 * H * N * PAIRS)
+
+F32 = mybir.dt.float32
+BF16 = mybir.dt.bfloat16
+I32 = mybir.dt.int32
+U32 = mybir.dt.uint32
+U16 = mybir.dt.uint16
+U8 = mybir.dt.uint8
+FP8X4 = mybir.dt.float8_e4m3fn_x4
+FP4X4 = mybir.dt.float4_e2m1fn_x4
+ALU = mybir.AluOpType
+ACT = mybir.ActivationFunctionType
+
+P = 128
+PACK = 4
+PASSES = K // (P * PACK)
+BANK = 512
+HALVES = S // BANK
+N_TILES = N // P
+LIST_ROWS = 16
+LIVE = 96
+PARTS = ((0, 256), (256, 128), (384, 128))
+
+
+def tile_list_motor_unit_readout_kernel(
+    tc, tab_words, tab_scales, offs, pos1, pos2, w1, w2_words, w2_scales, rest, gain, low, wa, wb_words, wb_scales, read, out
+):
+    nc = tc.nc
+    with ExitStack() as ctx:
+        keep = ctx.enter_context(tc.tile_pool(name="keep", bufs=1))
+        psum = ctx.enter_context(tc.psum_pool(name="psum", bufs=1))
+
+        def sb(name, shape, dtype, on=None):
+            return keep.tile(shape, dtype, name=name, tag=on or name, align_bytes=64)
+
+        def bank(index, shape, name):
+            return psum.tile(shape, F32, name=name, tag="bank%d" % index)
+
+        offs_sb = keep.tile([P, S // LIST_ROWS], U16, name="offs_sb")
+        pos_sb = [keep.tile([P, PAIRS // LIST_ROWS], U16, name="pos_sb%d" % i) for i in range(2)]
+
+        tab_sc = sb("tab_sc", [P, T], U8)
+        w2_sc_raw = sb("w2_sc_raw", [P, H], U8)
+        v_sc = sb("v_sc", [P, PASSES, S], U8)
+        w2_sc = sb("w2_sc", [P, PASSES, H], U8)
+        wb_sc = sb("wb_sc", [P, N], U8)
+        nc.vector.memset(w2_sc_raw[:LIVE, :].bitcast(I32), 0)
+        nc.vector.memset(tab_sc[:LIVE, :].bitcast(I32), 0)
+        nc.vector.memset(w2_sc[:].bitcast(I32), 0)
+        nc.vector.memset(v_sc[:].bitcast(I32), 0)
+        nc.vector.memset(wb_sc[:].bitcast(I32), 0)
+
+        tab = [sb("tab%d" % a, [P, T], U32) for a in range(PASSES)]
+        w2_raw = sb("w2_raw", [P, PASSES, 2 * H], U8)
+        w1_raw0 = sb("w1_raw0", [P, PACK, H], F32)
+        w1_raw1 = [sb("w1_raw1_%d" % u, [P, PACK, H // 2], F32) for u in range(2)]
+        rest_sb = [sb("rest%d" % t, [P, S], F32) for t in range(PACK)]
+        wa_raw = sb("wa_raw", [P, PACK, N], F32)
+        wb_codes = sb("wb_codes", [P, N], U32)
+        read_sb = sb("read_sb", [P, N_TILES, PAIRS], F32)
+
+        gain_sb = sb("gain_sb", [P, PACK], F32)
+        low_sb = sb("low_sb", [P, PACK], F32)
+
+        def table_words(a):
+            return tab_words[a].rearrange("p t i -> p (t i)").bitcast(I32)
+
+        w1_rows = w1.rearrange("(a p j) r -> a p j r", a=PASSES, j=PACK)
+        rest_rows = rest.rearrange("(p t) m -> p t m", t=PACK)
+        nc.sync.dma_start(offs_sb[:], offs)
+        nc.sync.dma_start(tab_sc[LIVE:, :].bitcast(I32), tab_scales.rearrange("a q t -> q a t").bitcast(I32))
+        nc.sync.dma_start(w2_sc_raw[LIVE:, :].bitcast(I32), w2_scales.rearrange("a q c -> q a c").bitcast(I32))
+        nc.sync.dma_start(tab[0][:].bitcast(I32), table_words(0))
+        nc.sync.dma_start(w2_raw[:].bitcast(I32), w2_words.rearrange("a p b -> p a b").bitcast(I32))
+        nc.sync.dma_start(w1_raw0[:], w1_rows[0])
+        nc.sync.dma_start(tab[1][:].bitcast(I32), table_words(1))
+        for u in range(2):
+            nc.sync.dma_start(w1_raw1[u][:], w1_rows[1][:, :, u * (H // 2) : (u + 1) * (H // 2)])
+        nc.sync.dma_start(rest_sb[0][:], rest_rows[:, 0, :])
+        nc.sync.dma_start(gain_sb[:], gain.rearrange("(p t) -> p t", t=PACK))
+        nc.sync.dma_start(pos_sb[0][:], pos1)
+        nc.sync.dma_start(pos_sb[1][:], pos2)
+        nc.sync.dma_start(low_sb[:], low.rearrange("(p t) -> p t", t=PACK))
+        for t in range(1, PACK):
+            nc.sync.dma_start(rest_sb[t][:], rest_rows[:, t, :])
+        nc.sync.dma_start(wa_raw[:], wa.rearrange("(p j) n -> p j n", j=PACK))
+        nc.sync.dma_start(wb_codes[:].bitcast(I32), wb_words[0].rearrange("p c i -> p (c i)").bitcast(I32))
+        nc.sync.dma_start(read_sb[:], read.rearrange("(i p) j -> p i j", p=P))
+
+        def to_planes(planes, rows):
+            for q in range(4):
+                nc.gpsimd.dma_start(
+                    planes[32 * q : 32 * q + 4, :, :].bitcast(I32), rows[LIVE + 8 * q : LIVE + 8 * (q + 1), :].bitcast(I32)
+                )
+
+        w2_sc_dealt = sb("w2_sc_dealt", [P, H], U8)
+        nc.vector.tensor_copy(
+            w2_sc_dealt[:].rearrange("p (t m) -> p m t", t=PACK), w2_sc_raw[:].rearrange("p (m t) -> p m t", t=PACK)
+        )
+        to_planes(w2_sc, w2_sc_dealt)
+        v_sc_rows = sb("v_sc_rows", [P, S], U8)
+        nc.vector.tensor_copy(v_sc_rows[:], tab_sc[:].indirect(offs_sb[:]))
+        to_planes(v_sc, v_sc_rows)
+
+        for q in range(4):
+            nc.gpsimd.dma_start(wb_sc[32 * q : 32 * q + 4, :].bitcast(I32), wb_scales[0, 4 * q : 4 * q + 4, :].bitcast(I32))
+
+        v_codes = [[sb("v_codes%d_%d" % (a, h), [P, BANK], U32) for h in range(HALVES)] for a in range(PASSES)]
+
+        def gather_words(a):
+            cols = BANK // LIST_ROWS
+            for h in range(HALVES):
+                nc.vector.tensor_copy(v_codes[a][h][:], tab[a][:].indirect(offs_sb[:, h * cols : (h + 1) * cols]))
+
+        gather_words(0)
+
+        w2_codes = sb("w2_codes", [P, PASSES, 2 * H], U8)
+        nc.vector.tensor_copy(
+            w2_codes[:].bitcast(U16).rearrange("p a (t m) -> p a m t", t=PACK),
+            w2_raw[:].bitcast(U16).rearrange("p a (m t) -> p a m t", t=PACK),
+        )
+
+        w1_bf = [sb("w1_bf%d" % a, [P, PACK, P, PACK], BF16) for a in range(PASSES)]
+        w1_codes = [sb("w1_codes%d" % a, [P, H], U32) for a in range(PASSES)]
+        w1_sc = [sb("w1_sc%d" % a, [P, H], U8) for a in range(PASSES)]
+
+        def dealt(a, m0, m1):
+            return w1_bf[a][:, :, m0:m1, :].rearrange("p t m j -> p m j t")
+
+        def by_line(raw):
+            return raw[:].rearrange("p j (m t) -> p m j t", t=PACK)
+
+        def quantise_w1(a):
+            nc.vector.quantize_mx(
+                out=w1_codes[a][:].bitcast(FP8X4), scales=w1_sc[a][:], in_=w1_bf[a][:].rearrange("p t m j -> p (t m j)")
+            )
+
+        nc.scalar.copy(dealt(0, 0, P), by_line(w1_raw0))
+        quantise_w1(0)
+        gather_words(1)
+        nc.scalar.copy(dealt(1, 0, P // 2), by_line(w1_raw1[0]))
+        nc.vector.tensor_copy(dealt(1, P // 2, P), by_line(w1_raw1[1]))
+        quantise_w1(1)
+
+        h_sb = [sb("h%d" % t, [P, S], F32) for t in range(PACK)]
+        picked = {}
+
+        def new_picked(g, on):
+            picked[g] = sb("picked%d" % g, [P, 2, PACK, PARTS[g][1]], F32, on=on)
+
+        def pick(g, t):
+            j0, w = PARTS[g]
+            cols = slice(j0 // LIST_ROWS, (j0 + w) // LIST_ROWS)
+            for i in (1, 0):
+                nc.vector.tensor_copy(picked[g][:, i, t, :], h_sb[t][:].indirect(pos_sb[i][:, cols]))
+            nc.vector.tensor_scalar(picked[g][:, 1, t, :], picked[g][:, 1, t, :], low_sb[:, t : t + 1], None, ALU.max)
+
+        new_picked(0, None)
+        for t in range(PACK):
+            rows = slice(t * P, (t + 1) * P)
+            cos_sb = sb("cos%d" % t, [P, S], F32)
+            for h in range(HALVES):
+                cols = slice(h * BANK, (h + 1) * BANK)
+                phase = bank(4 + (HALVES * t + h) % 4, [P, BANK], "phase")
+                for a in range(PASSES):
+                    nc.tensor.matmul_mx(
+                        out=phase[:],
+                        lhsT=w2_codes[:, a, 2 * t * P : 2 * (t + 1) * P].bitcast(FP4X4),
+                        lhsT_scale=w2_sc[:, a, rows],
+                        rhs=v_codes[a][h][:].bitcast(FP8X4),
+                        rhs_scale=v_sc[:, a, cols],
+                        start=(a == 0),
+                        stop=(a == PASSES - 1),
+                    )
+                nc.scalar.activation(cos_sb[:, cols], phase[:], ACT.Abs)
+            nc.scalar.activation(cos_sb[:], cos_sb[:], ACT.Sin, bias=math.pi / 2, scale=-1.0)
+            for h in range(HALVES):
+                cols = slice(h * BANK, (h + 1) * BANK)
+                shape_ps = bank((HALVES * t + h) % 4, [P, BANK], "shape_ps")
+                for a in range(PASSES):
+                    nc.tensor.matmul_mx(
+                        out=shape_ps[:],
+                        lhsT=w1_codes[a][:, rows].bitcast(FP8X4),
+                        lhsT_scale=w1_sc[a][:, rows],
+                        rhs=v_codes[a][h][:].bitcast(FP8X4),
+                        rhs_scale=v_sc[:, a, cols],
+                        start=(a == 0),
+                        stop=(a == PASSES - 1),
+                    )
+                nc.vector.tensor_tensor(h_sb[t][:, cols], shape_ps[:], rest_sb[t][:, cols], ALU.add)
+            nc.vector.scalar_tensor_tensor(h_sb[t][:], h_sb[t][:], gain_sb[:, t : t + 1], cos_sb[:], ALU.mult, ALU.mult)
+            pick(0, t)
+
+        wa_codes = sb("wa_codes", [P, N], U32)
+        wa_sc = sb("wa_sc", [P, N], U8)
+        for u in range(2):
+            cols = slice(u * (N // 2), (u + 1) * (N // 2))
+            wa_bf = sb("wa_bf%d" % u, [P, N // 2, PACK], BF16, on="rest%d" % (u + 1))
+            nc.scalar.copy(
+                wa_bf[:].rearrange("p (c i) j -> p c j i", i=4), wa_raw[:, :, cols].rearrange("p j (c i) -> p c j i", i=4)
+            )
+            nc.vector.quantize_mx(
+                out=wa_codes[:, cols].bitcast(FP8X4), scales=wa_sc[:, cols], in_=wa_bf[:].rearrange("p c j -> p (c j)")
+            )
+
+        out_rows = out.rearrange("(i p) j -> p i j", p=P)
+        y_banks = ((4, 5, 6), (7, 0), (1, 2))
+        for g, (j0, w) in enumerate(PARTS):
+            if g > 0:
+                new_picked(g, "cos3" if g == 1 else "x_bf0")
+                for t in range(PACK):
+                    pick(g, t)
+            x_bf = sb("x_bf%d" % g, [P, 2, w, PACK], BF16)
+            x_codes = sb("x_codes%d" % g, [P, 2, w], U32)
+            x_sc = sb("x_sc%d" % g, [P, 2, w], U8)
+            woven = [x_bf[:, i, :, :].rearrange("p (c i) t -> p c t i", i=4) for i in range(2)]
+            planes = [picked[g][:, i, :, :].rearrange("p t (c i) -> p c t i", i=4) for i in range(2)]
+            nc.scalar.copy(woven[1], planes[1])
+            nc.scalar.activation(woven[0], planes[0], ACT.Abs)
+            nc.vector.quantize_mx(
+                out=x_codes[:].rearrange("p i w -> p (i w)").bitcast(FP8X4),
+                scales=x_sc[:].rearrange("p i w -> p (i w)"),
+                in_=x_bf[:].rearrange("p i w t -> p (i w t)"),
+            )
+            result = sb("result%d" % g, [P, N_TILES, w], F32)
+            per_bank = N_TILES // len(y_banks[g])
+            for b, index in enumerate(y_banks[g]):
+                y = bank(index, [P, per_bank, w], "y")
+                tiles = slice(b * per_bank, (b + 1) * per_bank)
+                for e in range(per_bank):
+                    cols = slice((b * per_bank + e) * P, (b * per_bank + e + 1) * P)
+                    for i, (codes, scales) in enumerate(((wa_codes, wa_sc), (wb_codes, wb_sc))):
+                        nc.tensor.matmul_mx(
+                            out=y[:, e, :],
+                            lhsT=codes[:, cols].bitcast(FP8X4),
+                            lhsT_scale=scales[:, cols],
+                            rhs=x_codes[:, i, :].bitcast(FP8X4),
+                            rhs_scale=x_sc[:, i, :],
+                            start=(i == 0),
+                            stop=(i == 1),
+                        )
+                nc.vector.tensor_tensor(result[:, tiles, :], y[:], read_sb[:, tiles, j0 : j0 + w], ALU.mult)
+                nc.sync.dma_start(out_rows[:, tiles, j0 : j0 + w], result[:, tiles, :])

@@ -25,7 +25,10 @@ HALVES = S // BANK
 N_TILES = N // P
 LIST_ROWS = 16
 LIVE = 96
-PARTS = ((0, 256), (256, 128), (384, 128))
+PARTS = 2
+WIDTH = PAIRS // PARTS
+V_AT, W2_AT, WB_AT, SC_WIDTH = 0, S, S + H, S + H + N // 2
+EARLY, LATE = 0, 1
 
 
 def tile_list_motor_unit_readout_kernel(
@@ -47,14 +50,11 @@ def tile_list_motor_unit_readout_kernel(
 
         tab_sc = sb("tab_sc", [P, T], U8)
         w2_sc_raw = sb("w2_sc_raw", [P, H], U8)
-        v_sc = sb("v_sc", [P, PASSES, S], U8)
-        w2_sc = sb("w2_sc", [P, PASSES, H], U8)
-        wb_sc = sb("wb_sc", [P, N], U8)
+        sc_rows = sb("sc_rows", [P, SC_WIDTH], U8)
+        planes = sb("planes", [P, PASSES, SC_WIDTH], U8)
         nc.vector.memset(w2_sc_raw[:LIVE, :].bitcast(I32), 0)
         nc.vector.memset(tab_sc[:LIVE, :].bitcast(I32), 0)
-        nc.vector.memset(w2_sc[:].bitcast(I32), 0)
-        nc.vector.memset(v_sc[:].bitcast(I32), 0)
-        nc.vector.memset(wb_sc[:].bitcast(I32), 0)
+        nc.vector.memset(planes[:].bitcast(I32), 0)
 
         tab = [sb("tab%d" % a, [P, T], U32) for a in range(PASSES)]
         w2_raw = sb("w2_raw", [P, PASSES, 2 * H], U8)
@@ -64,7 +64,6 @@ def tile_list_motor_unit_readout_kernel(
         wa_raw = sb("wa_raw", [P, PACK, N], F32)
         wb_codes = sb("wb_codes", [P, N], U32)
         read_sb = sb("read_sb", [P, N_TILES, PAIRS], F32)
-
         gain_sb = sb("gain_sb", [P, PACK], F32)
         low_sb = sb("low_sb", [P, PACK], F32)
 
@@ -76,6 +75,7 @@ def tile_list_motor_unit_readout_kernel(
         nc.sync.dma_start(offs_sb[:], offs)
         nc.sync.dma_start(tab_sc[LIVE:, :].bitcast(I32), tab_scales.rearrange("a q t -> q a t").bitcast(I32))
         nc.sync.dma_start(w2_sc_raw[LIVE:, :].bitcast(I32), w2_scales.rearrange("a q c -> q a c").bitcast(I32))
+        nc.sync.dma_start(sc_rows[LIVE:, WB_AT:].bitcast(I32), wb_scales[0].rearrange("q (a c) -> (q a) c", a=2).bitcast(I32))
         nc.sync.dma_start(tab[0][:].bitcast(I32), table_words(0))
         nc.sync.dma_start(w2_raw[:].bitcast(I32), w2_words.rearrange("a p b -> p a b").bitcast(I32))
         nc.sync.dma_start(w1_raw0[:], w1_rows[0])
@@ -84,8 +84,8 @@ def tile_list_motor_unit_readout_kernel(
             nc.sync.dma_start(w1_raw1[u][:], w1_rows[1][:, :, u * (H // 2) : (u + 1) * (H // 2)])
         nc.sync.dma_start(rest_sb[0][:], rest_rows[:, 0, :])
         nc.sync.dma_start(gain_sb[:], gain.rearrange("(p t) -> p t", t=PACK))
-        nc.sync.dma_start(pos_sb[0][:], pos1)
-        nc.sync.dma_start(pos_sb[1][:], pos2)
+        nc.sync.dma_start(pos_sb[EARLY][:], pos1)
+        nc.sync.dma_start(pos_sb[LATE][:], pos2)
         nc.sync.dma_start(low_sb[:], low.rearrange("(p t) -> p t", t=PACK))
         for t in range(1, PACK):
             nc.sync.dma_start(rest_sb[t][:], rest_rows[:, t, :])
@@ -93,23 +93,16 @@ def tile_list_motor_unit_readout_kernel(
         nc.sync.dma_start(wb_codes[:].bitcast(I32), wb_words[0].rearrange("p c i -> p (c i)").bitcast(I32))
         nc.sync.dma_start(read_sb[:], read.rearrange("(i p) j -> p i j", p=P))
 
-        def to_planes(planes, rows):
-            for q in range(4):
-                nc.gpsimd.dma_start(
-                    planes[32 * q : 32 * q + 4, :, :].bitcast(I32), rows[LIVE + 8 * q : LIVE + 8 * (q + 1), :].bitcast(I32)
-                )
-
-        w2_sc_dealt = sb("w2_sc_dealt", [P, H], U8)
         nc.vector.tensor_copy(
-            w2_sc_dealt[:].rearrange("p (t m) -> p m t", t=PACK), w2_sc_raw[:].rearrange("p (m t) -> p m t", t=PACK)
+            sc_rows[:, W2_AT:WB_AT].rearrange("p (t m) -> p t m", t=PACK), w2_sc_raw[:].rearrange("p (m t) -> p t m", t=PACK)
         )
-        to_planes(w2_sc, w2_sc_dealt)
         v_sc_rows = sb("v_sc_rows", [P, S], U8)
         nc.vector.tensor_copy(v_sc_rows[:], tab_sc[:].indirect(offs_sb[:]))
-        to_planes(v_sc, v_sc_rows)
-
+        nc.vector.tensor_copy(sc_rows[LIVE:, V_AT:W2_AT].bitcast(I32), v_sc_rows[LIVE:, :].bitcast(I32))
         for q in range(4):
-            nc.gpsimd.dma_start(wb_sc[32 * q : 32 * q + 4, :].bitcast(I32), wb_scales[0, 4 * q : 4 * q + 4, :].bitcast(I32))
+            nc.gpsimd.dma_start(
+                planes[32 * q : 32 * q + 4, :, :].bitcast(I32), sc_rows[LIVE + 8 * q : LIVE + 8 * (q + 1), :].bitcast(I32)
+            )
 
         v_codes = [[sb("v_codes%d_%d" % (a, h), [P, BANK], U32) for h in range(HALVES)] for a in range(PASSES)]
 
@@ -122,8 +115,8 @@ def tile_list_motor_unit_readout_kernel(
 
         w2_codes = sb("w2_codes", [P, PASSES, 2 * H], U8)
         nc.vector.tensor_copy(
-            w2_codes[:].bitcast(U16).rearrange("p a (t m) -> p a m t", t=PACK),
-            w2_raw[:].bitcast(U16).rearrange("p a (m t) -> p a m t", t=PACK),
+            w2_codes[:].bitcast(U16).rearrange("p a (t m) -> p a t m", t=PACK),
+            w2_raw[:].bitcast(U16).rearrange("p a (m t) -> p a t m", t=PACK),
         )
 
         w1_bf = [sb("w1_bf%d" % a, [P, PACK, P, PACK], BF16) for a in range(PASSES)]
@@ -131,10 +124,10 @@ def tile_list_motor_unit_readout_kernel(
         w1_sc = [sb("w1_sc%d" % a, [P, H], U8) for a in range(PASSES)]
 
         def dealt(a, m0, m1):
-            return w1_bf[a][:, :, m0:m1, :].rearrange("p t m j -> p m j t")
+            return w1_bf[a][:, :, m0:m1, :].rearrange("p t m j -> p m t j")
 
         def by_line(raw):
-            return raw[:].rearrange("p j (m t) -> p m j t", t=PACK)
+            return raw[:].rearrange("p j (m t) -> p m t j", t=PACK)
 
         def quantise_w1(a):
             nc.vector.quantize_mx(
@@ -149,57 +142,59 @@ def tile_list_motor_unit_readout_kernel(
         quantise_w1(1)
 
         h_sb = [sb("h%d" % t, [P, S], F32) for t in range(PACK)]
+        cos_sb = [sb("cos%d" % t, [P, S], F32) for t in range(PACK)]
+        shape_ps = {}
+
+        def table_product(acc, h, weights):
+            for a in range(PASSES):
+                codes, scales = weights(a)
+                nc.tensor.matmul_mx(
+                    out=acc[:],
+                    lhsT=codes,
+                    lhsT_scale=scales,
+                    rhs=v_codes[a][h][:].bitcast(FP8X4),
+                    rhs_scale=planes[:, a, V_AT + h * BANK : V_AT + (h + 1) * BANK],
+                    start=(a == 0),
+                    stop=(a == PASSES - 1),
+                )
+
+        def cosine(t):
+            for h in range(HALVES):
+                phase = bank(4 + (HALVES * t + h) % 4, [P, BANK], "phase")
+                table_product(
+                    phase,
+                    h,
+                    lambda a: (
+                        w2_codes[:, a, 2 * t * P : 2 * (t + 1) * P].bitcast(FP4X4),
+                        planes[:, a, W2_AT + t * P : W2_AT + (t + 1) * P],
+                    ),
+                )
+                nc.scalar.activation(cos_sb[t][:, h * BANK : (h + 1) * BANK], phase[:], ACT.Abs)
+            nc.scalar.activation(cos_sb[t][:], cos_sb[t][:], ACT.Sin, bias=math.pi / 2, scale=-1.0)
+
+        def shape_product(t):
+            rows = slice(t * P, (t + 1) * P)
+            for h in range(HALVES):
+                shape_ps[t, h] = bank((HALVES * t + h) % 4, [P, BANK], "shape_ps")
+                table_product(shape_ps[t, h], h, lambda a: (w1_codes[a][:, rows].bitcast(FP8X4), w1_sc[a][:, rows]))
+
+        def add_rest(t, h):
+            cols = slice(h * BANK, (h + 1) * BANK)
+            nc.vector.tensor_tensor(h_sb[t][:, cols], shape_ps[t, h][:], rest_sb[t][:, cols], ALU.add)
+
         picked = {}
 
-        def new_picked(g, on):
-            picked[g] = sb("picked%d" % g, [P, 2, PACK, PARTS[g][1]], F32, on=on)
+        def pick(g, i, t):
+            cols = slice(g * WIDTH // LIST_ROWS, (g + 1) * WIDTH // LIST_ROWS)
+            nc.vector.tensor_copy(picked[g, i][:, t, :], h_sb[t][:].indirect(pos_sb[i][:, cols]))
 
-        def pick(g, t):
-            j0, w = PARTS[g]
-            cols = slice(j0 // LIST_ROWS, (j0 + w) // LIST_ROWS)
-            for i in (1, 0):
-                nc.vector.tensor_copy(picked[g][:, i, t, :], h_sb[t][:].indirect(pos_sb[i][:, cols]))
-            nc.vector.tensor_scalar(picked[g][:, 1, t, :], picked[g][:, 1, t, :], low_sb[:, t : t + 1], None, ALU.max)
-
-        new_picked(0, None)
-        for t in range(PACK):
-            rows = slice(t * P, (t + 1) * P)
-            cos_sb = sb("cos%d" % t, [P, S], F32)
-            for h in range(HALVES):
-                cols = slice(h * BANK, (h + 1) * BANK)
-                phase = bank(4 + (HALVES * t + h) % 4, [P, BANK], "phase")
-                for a in range(PASSES):
-                    nc.tensor.matmul_mx(
-                        out=phase[:],
-                        lhsT=w2_codes[:, a, 2 * t * P : 2 * (t + 1) * P].bitcast(FP4X4),
-                        lhsT_scale=w2_sc[:, a, rows],
-                        rhs=v_codes[a][h][:].bitcast(FP8X4),
-                        rhs_scale=v_sc[:, a, cols],
-                        start=(a == 0),
-                        stop=(a == PASSES - 1),
-                    )
-                nc.scalar.activation(cos_sb[:, cols], phase[:], ACT.Abs)
-            nc.scalar.activation(cos_sb[:], cos_sb[:], ACT.Sin, bias=math.pi / 2, scale=-1.0)
-            for h in range(HALVES):
-                cols = slice(h * BANK, (h + 1) * BANK)
-                shape_ps = bank((HALVES * t + h) % 4, [P, BANK], "shape_ps")
-                for a in range(PASSES):
-                    nc.tensor.matmul_mx(
-                        out=shape_ps[:],
-                        lhsT=w1_codes[a][:, rows].bitcast(FP8X4),
-                        lhsT_scale=w1_sc[a][:, rows],
-                        rhs=v_codes[a][h][:].bitcast(FP8X4),
-                        rhs_scale=v_sc[:, a, cols],
-                        start=(a == 0),
-                        stop=(a == PASSES - 1),
-                    )
-                nc.vector.tensor_tensor(h_sb[t][:, cols], shape_ps[:], rest_sb[t][:, cols], ALU.add)
-            nc.vector.scalar_tensor_tensor(h_sb[t][:], h_sb[t][:], gain_sb[:, t : t + 1], cos_sb[:], ALU.mult, ALU.mult)
-            pick(0, t)
+        def bound_below(g, t):
+            nc.vector.tensor_scalar(picked[g, LATE][:, t, :], picked[g, LATE][:, t, :], low_sb[:, t : t + 1], None, ALU.max)
 
         wa_codes = sb("wa_codes", [P, N], U32)
         wa_sc = sb("wa_sc", [P, N], U8)
-        for u in range(2):
+
+        def quantise_wa(u):
             cols = slice(u * (N // 2), (u + 1) * (N // 2))
             wa_bf = sb("wa_bf%d" % u, [P, N // 2, PACK], BF16, on="rest%d" % (u + 1))
             nc.scalar.copy(
@@ -209,41 +204,83 @@ def tile_list_motor_unit_readout_kernel(
                 out=wa_codes[:, cols].bitcast(FP8X4), scales=wa_sc[:, cols], in_=wa_bf[:].rearrange("p c j -> p (c j)")
             )
 
+        for i in (EARLY, LATE):
+            picked[0, i] = sb("picked0_%d" % i, [P, PACK, WIDTH], F32)
+        for t in range(2):
+            cosine(t)
+        for t in range(2):
+            shape_product(t)
+        for h in range(HALVES):
+            add_rest(0, h)
+        for t in range(PACK):
+            if t + 2 < PACK:
+                cosine(t + 2)
+                shape_product(t + 2)
+            if t + 1 < PACK:
+                add_rest(t + 1, 0)
+            nc.vector.scalar_tensor_tensor(h_sb[t][:], h_sb[t][:], gain_sb[:, t : t + 1], cos_sb[t][:], ALU.mult, ALU.mult)
+            if t + 1 < PACK:
+                add_rest(t + 1, 1)
+            if t >= 2:
+                quantise_wa(t - 2)
+            pick(0, LATE, t)
+            pick(0, EARLY, t)
+            bound_below(0, t)
+
         out_rows = out.rearrange("(i p) j -> p i j", p=P)
-        y_banks = ((4, 5, 6), (7, 0), (1, 2))
-        for g, (j0, w) in enumerate(PARTS):
-            if g > 0:
-                new_picked(g, "cos3" if g == 1 else "x_bf0")
+        y_banks = ((4, 5, 6), (7, 0, 1))
+        per_bank = BANK // WIDTH
+
+        def weave(g, i, x_bf):
+            woven = x_bf[:, i, :, :].rearrange("p (c e) t -> p c t e", e=4)
+            source = picked[g, i][:].rearrange("p t (c e) -> p c t e", e=4)
+            if i == EARLY:
+                nc.scalar.activation(woven, source, ACT.Abs)
+            else:
+                nc.scalar.copy(woven, source)
+
+        for g in range(PARTS):
+            x_bf = sb("x_bf%d" % g, [P, 2, WIDTH, PACK], BF16)
+            x_codes = sb("x_codes%d" % g, [P, 2, WIDTH], U32)
+            x_sc = sb("x_sc%d" % g, [P, 2, WIDTH], U8)
+            if g == 0:
+                weave(g, LATE, x_bf)
+                weave(g, EARLY, x_bf)
+            else:
+                picked[g, EARLY] = sb("picked1_0", [P, PACK, WIDTH], F32, on="cos%d" % (PACK - 1))
+                picked[g, LATE] = sb("picked1_1", [P, PACK, WIDTH], F32, on="x_bf0")
                 for t in range(PACK):
-                    pick(g, t)
-            x_bf = sb("x_bf%d" % g, [P, 2, w, PACK], BF16)
-            x_codes = sb("x_codes%d" % g, [P, 2, w], U32)
-            x_sc = sb("x_sc%d" % g, [P, 2, w], U8)
-            woven = [x_bf[:, i, :, :].rearrange("p (c i) t -> p c t i", i=4) for i in range(2)]
-            planes = [picked[g][:, i, :, :].rearrange("p t (c i) -> p c t i", i=4) for i in range(2)]
-            nc.scalar.copy(woven[1], planes[1])
-            nc.scalar.activation(woven[0], planes[0], ACT.Abs)
+                    pick(g, EARLY, t)
+                weave(g, EARLY, x_bf)
+                for t in range(PACK):
+                    pick(g, LATE, t)
+                for t in range(PACK):
+                    bound_below(g, t)
+                weave(g, LATE, x_bf)
             nc.vector.quantize_mx(
                 out=x_codes[:].rearrange("p i w -> p (i w)").bitcast(FP8X4),
                 scales=x_sc[:].rearrange("p i w -> p (i w)"),
                 in_=x_bf[:].rearrange("p i w t -> p (i w t)"),
             )
-            result = sb("result%d" % g, [P, N_TILES, w], F32)
-            per_bank = N_TILES // len(y_banks[g])
+            pairs = slice(g * WIDTH, (g + 1) * WIDTH)
             for b, index in enumerate(y_banks[g]):
-                y = bank(index, [P, per_bank, w], "y")
+                y = bank(index, [P, per_bank, WIDTH], "y")
                 tiles = slice(b * per_bank, (b + 1) * per_bank)
                 for e in range(per_bank):
-                    cols = slice((b * per_bank + e) * P, (b * per_bank + e + 1) * P)
-                    for i, (codes, scales) in enumerate(((wa_codes, wa_sc), (wb_codes, wb_sc))):
+                    n_tile = b * per_bank + e
+                    cols = slice(n_tile * P, (n_tile + 1) * P)
+                    wb_at = WB_AT + (n_tile % (N_TILES // 2)) * P
+                    weights = ((wa_codes, wa_sc[:, cols]), (wb_codes, planes[:, n_tile // (N_TILES // 2), wb_at : wb_at + P]))
+                    for i, (codes, scales) in enumerate(weights):
                         nc.tensor.matmul_mx(
                             out=y[:, e, :],
                             lhsT=codes[:, cols].bitcast(FP8X4),
-                            lhsT_scale=scales[:, cols],
+                            lhsT_scale=scales,
                             rhs=x_codes[:, i, :].bitcast(FP8X4),
                             rhs_scale=x_sc[:, i, :],
                             start=(i == 0),
                             stop=(i == 1),
                         )
-                nc.vector.tensor_tensor(result[:, tiles, :], y[:], read_sb[:, tiles, j0 : j0 + w], ALU.mult)
-                nc.sync.dma_start(out_rows[:, tiles, j0 : j0 + w], result[:, tiles, :])
+                result = sb("result%d_%d" % (g, b), [P, per_bank, WIDTH], F32)
+                nc.vector.tensor_tensor(result[:], y[:], read_sb[:, tiles, pairs], ALU.mult)
+                nc.sync.dma_start(out_rows[:, tiles, pairs], result[:])

@@ -56,6 +56,10 @@ def tile_list_motor_unit_readout_kernel(
         nc.vector.memset(tab_sc[:LIVE, :].bitcast(I32), 0)
         nc.vector.memset(planes[:].bitcast(I32), 0)
 
+        warm = sb("warm", [P, 1], F32)
+        nc.vector.memset(warm[:], 0.0)
+        nc.scalar.activation(warm[:], warm[:], ACT.Sin)
+
         tab = [sb("tab%d" % a, [P, T], U32) for a in range(PASSES)]
         w2_raw = sb("w2_raw", [P, PASSES, 2 * H], U8)
         w1_raw0 = sb("w1_raw0", [P, PACK, H], F32)
@@ -76,9 +80,9 @@ def tile_list_motor_unit_readout_kernel(
         nc.sync.dma_start(tab_sc[LIVE:, :].bitcast(I32), tab_scales.rearrange("a q t -> q a t").bitcast(I32))
         nc.sync.dma_start(w2_sc_raw[LIVE:, :].bitcast(I32), w2_scales.rearrange("a q c -> q a c").bitcast(I32))
         nc.sync.dma_start(sc_rows[LIVE:, WB_AT:].bitcast(I32), wb_scales[0].rearrange("q (a c) -> (q a) c", a=2).bitcast(I32))
+        nc.sync.dma_start(w1_raw0[:], w1_rows[0])
         nc.sync.dma_start(tab[0][:].bitcast(I32), table_words(0))
         nc.sync.dma_start(w2_raw[:].bitcast(I32), w2_words.rearrange("a p b -> p a b").bitcast(I32))
-        nc.sync.dma_start(w1_raw0[:], w1_rows[0])
         nc.sync.dma_start(tab[1][:].bitcast(I32), table_words(1))
         for u in range(2):
             nc.sync.dma_start(w1_raw1[u][:], w1_rows[1][:, :, u * (H // 2) : (u + 1) * (H // 2)])
@@ -111,14 +115,6 @@ def tile_list_motor_unit_readout_kernel(
             for h in range(HALVES):
                 nc.vector.tensor_copy(v_codes[a][h][:], tab[a][:].indirect(offs_sb[:, h * cols : (h + 1) * cols]))
 
-        gather_words(0)
-
-        w2_codes = sb("w2_codes", [P, PASSES, 2 * H], U8)
-        nc.vector.tensor_copy(
-            w2_codes[:].bitcast(U16).rearrange("p a (t m) -> p a t m", t=PACK),
-            w2_raw[:].bitcast(U16).rearrange("p a (m t) -> p a t m", t=PACK),
-        )
-
         w1_bf = [sb("w1_bf%d" % a, [P, PACK, P, PACK], BF16) for a in range(PASSES)]
         w1_codes = [sb("w1_codes%d" % a, [P, H], U32) for a in range(PASSES)]
         w1_sc = [sb("w1_sc%d" % a, [P, H], U8) for a in range(PASSES)]
@@ -129,20 +125,32 @@ def tile_list_motor_unit_readout_kernel(
         def by_line(raw):
             return raw[:].rearrange("p j (m t) -> p m t j", t=PACK)
 
-        def quantise_w1(a):
+        def quantise_w1(a, t0, t1):
+            cols = slice(t0 * P, t1 * P)
             nc.vector.quantize_mx(
-                out=w1_codes[a][:].bitcast(FP8X4), scales=w1_sc[a][:], in_=w1_bf[a][:].rearrange("p t m j -> p (t m j)")
+                out=w1_codes[a][:, cols].bitcast(FP8X4),
+                scales=w1_sc[a][:, cols],
+                in_=w1_bf[a][:, t0:t1, :, :].rearrange("p t m j -> p (t m j)"),
             )
 
         nc.scalar.copy(dealt(0, 0, P), by_line(w1_raw0))
-        quantise_w1(0)
+        quantise_w1(0, 0, PACK)
+        gather_words(0)
+
+        w2_codes = sb("w2_codes", [P, PASSES, 2 * H], U8)
+        nc.vector.tensor_copy(
+            w2_codes[:].bitcast(U16).rearrange("p a (t m) -> p a t m", t=PACK),
+            w2_raw[:].bitcast(U16).rearrange("p a (m t) -> p a t m", t=PACK),
+        )
+
         gather_words(1)
         nc.scalar.copy(dealt(1, 0, P // 2), by_line(w1_raw1[0]))
         nc.vector.tensor_copy(dealt(1, P // 2, P), by_line(w1_raw1[1]))
-        quantise_w1(1)
+        quantise_w1(1, 0, 1)
+        quantise_w1(1, 1, PACK)
 
         h_sb = [sb("h%d" % t, [P, S], F32) for t in range(PACK)]
-        cos_sb = [sb("cos%d" % t, [P, S], F32) for t in range(PACK)]
+        cos_sb = [sb("cos%d" % t, [P, S], F32, on="w1_raw1_0" if t == 0 else None) for t in range(PACK)]
         shape_ps = {}
 
         def table_product(acc, h, weights):
@@ -194,14 +202,13 @@ def tile_list_motor_unit_readout_kernel(
         wa_codes = sb("wa_codes", [P, N], U32)
         wa_sc = sb("wa_sc", [P, N], U8)
 
-        def quantise_wa(u):
+        def quantise_wa(wa_bf, u):
             cols = slice(u * (N // 2), (u + 1) * (N // 2))
-            wa_bf = sb("wa_bf%d" % u, [P, N // 2, PACK], BF16, on="rest%d" % (u + 1))
             nc.scalar.copy(
-                wa_bf[:].rearrange("p (c i) j -> p c j i", i=4), wa_raw[:, :, cols].rearrange("p j (c i) -> p c j i", i=4)
+                wa_bf[:, cols, :].rearrange("p (c i) j -> p c j i", i=4), wa_raw[:, :, cols].rearrange("p j (c i) -> p c j i", i=4)
             )
             nc.vector.quantize_mx(
-                out=wa_codes[:, cols].bitcast(FP8X4), scales=wa_sc[:, cols], in_=wa_bf[:].rearrange("p c j -> p (c j)")
+                out=wa_codes[:, cols].bitcast(FP8X4), scales=wa_sc[:, cols], in_=wa_bf[:, cols, :].rearrange("p c j -> p (c j)")
             )
 
         for i in (EARLY, LATE):
@@ -221,66 +228,72 @@ def tile_list_motor_unit_readout_kernel(
             nc.vector.scalar_tensor_tensor(h_sb[t][:], h_sb[t][:], gain_sb[:, t : t + 1], cos_sb[t][:], ALU.mult, ALU.mult)
             if t + 1 < PACK:
                 add_rest(t + 1, 1)
-            if t >= 2:
-                quantise_wa(t - 2)
             pick(0, LATE, t)
             pick(0, EARLY, t)
             bound_below(0, t)
+
+        wa_bf = sb("wa_bf", [P, N, PACK], BF16, on="rest%d" % (PACK - 1))
+        for u in range(2):
+            quantise_wa(wa_bf, u)
 
         out_rows = out.rearrange("(i p) j -> p i j", p=P)
         y_banks = ((4, 5, 6), (7, 0, 1))
         per_bank = BANK // WIDTH
 
-        def weave(g, i, x_bf):
-            woven = x_bf[:, i, :, :].rearrange("p (c e) t -> p c t e", e=4)
+        x_codes, x_sc = {}, {}
+
+        def quantise_x(g, i):
+            x_bf = sb("x_bf%d_%d" % (g, i), [P, WIDTH, PACK], BF16)
+            x_codes[g, i] = sb("x_codes%d_%d" % (g, i), [P, WIDTH], U32)
+            x_sc[g, i] = sb("x_sc%d_%d" % (g, i), [P, WIDTH], U8)
+            woven = x_bf[:].rearrange("p (c e) t -> p c t e", e=4)
             source = picked[g, i][:].rearrange("p t (c e) -> p c t e", e=4)
             if i == EARLY:
                 nc.scalar.activation(woven, source, ACT.Abs)
             else:
                 nc.scalar.copy(woven, source)
+            nc.vector.quantize_mx(
+                out=x_codes[g, i][:].bitcast(FP8X4), scales=x_sc[g, i][:], in_=x_bf[:].rearrange("p w t -> p (w t)")
+            )
+
+        def product(g, i, y, b, first):
+            for e in range(per_bank):
+                n_tile = b * per_bank + e
+                cols = slice(n_tile * P, (n_tile + 1) * P)
+                if i == EARLY:
+                    codes, scales = wa_codes[:, cols], wa_sc[:, cols]
+                else:
+                    wb_at = WB_AT + (n_tile % (N_TILES // 2)) * P
+                    codes, scales = wb_codes[:, cols], planes[:, n_tile // (N_TILES // 2), wb_at : wb_at + P]
+                nc.tensor.matmul_mx(
+                    out=y[:, e, :],
+                    lhsT=codes.bitcast(FP8X4),
+                    lhsT_scale=scales,
+                    rhs=x_codes[g, i][:].bitcast(FP8X4),
+                    rhs_scale=x_sc[g, i][:],
+                    start=(first and e == 0),
+                    stop=(not first and e == per_bank - 1),
+                )
 
         for g in range(PARTS):
-            x_bf = sb("x_bf%d" % g, [P, 2, WIDTH, PACK], BF16)
-            x_codes = sb("x_codes%d" % g, [P, 2, WIDTH], U32)
-            x_sc = sb("x_sc%d" % g, [P, 2, WIDTH], U8)
-            if g == 0:
-                weave(g, LATE, x_bf)
-                weave(g, EARLY, x_bf)
-            else:
-                picked[g, EARLY] = sb("picked1_0", [P, PACK, WIDTH], F32, on="cos%d" % (PACK - 1))
-                picked[g, LATE] = sb("picked1_1", [P, PACK, WIDTH], F32, on="x_bf0")
-                for t in range(PACK):
-                    pick(g, EARLY, t)
-                weave(g, EARLY, x_bf)
-                for t in range(PACK):
-                    pick(g, LATE, t)
-                for t in range(PACK):
-                    bound_below(g, t)
-                weave(g, LATE, x_bf)
-            nc.vector.quantize_mx(
-                out=x_codes[:].rearrange("p i w -> p (i w)").bitcast(FP8X4),
-                scales=x_sc[:].rearrange("p i w -> p (i w)"),
-                in_=x_bf[:].rearrange("p i w t -> p (i w t)"),
-            )
+            ys = [bank(index, [P, per_bank, WIDTH], "y") for index in y_banks[g]]
+            order = (LATE, EARLY) if g == 0 else (EARLY, LATE)
+            for i in order:
+                if g > 0:
+                    picked[g, i] = sb("picked1_%d" % i, [P, PACK, WIDTH], F32, on="cos3" if i == EARLY else "x_bf0_0")
+                    for t in range(PACK):
+                        pick(g, i, t)
+                    if i == LATE:
+                        for t in range(PACK):
+                            bound_below(g, t)
+                quantise_x(g, i)
+                if i == order[0]:
+                    for b, y in enumerate(ys):
+                        product(g, i, y, b, True)
             pairs = slice(g * WIDTH, (g + 1) * WIDTH)
-            for b, index in enumerate(y_banks[g]):
-                y = bank(index, [P, per_bank, WIDTH], "y")
+            for b, y in enumerate(ys):
                 tiles = slice(b * per_bank, (b + 1) * per_bank)
-                for e in range(per_bank):
-                    n_tile = b * per_bank + e
-                    cols = slice(n_tile * P, (n_tile + 1) * P)
-                    wb_at = WB_AT + (n_tile % (N_TILES // 2)) * P
-                    weights = ((wa_codes, wa_sc[:, cols]), (wb_codes, planes[:, n_tile // (N_TILES // 2), wb_at : wb_at + P]))
-                    for i, (codes, scales) in enumerate(weights):
-                        nc.tensor.matmul_mx(
-                            out=y[:, e, :],
-                            lhsT=codes[:, cols].bitcast(FP8X4),
-                            lhsT_scale=scales,
-                            rhs=x_codes[:, i, :].bitcast(FP8X4),
-                            rhs_scale=x_sc[:, i, :],
-                            start=(i == 0),
-                            stop=(i == 1),
-                        )
+                product(g, order[1], y, b, False)
                 result = sb("result%d_%d" % (g, b), [P, per_bank, WIDTH], F32)
                 nc.vector.tensor_tensor(result[:], y[:], read_sb[:, tiles, pairs], ALU.mult)
                 nc.sync.dma_start(out_rows[:, tiles, pairs], result[:])

@@ -60,42 +60,30 @@ def tile_list_motor_unit_readout_kernel(
         nc.vector.memset(warm[:], 0.0)
         nc.scalar.activation(warm[:], warm[:], ACT.Sin)
 
-        tab = [sb("tab%d" % a, [P, T], U32) for a in range(PASSES)]
-        w2_raw = sb("w2_raw", [P, PASSES, 2 * H], U8)
-        w1_raw0 = sb("w1_raw0", [P, PACK, H], F32)
-        w1_raw1 = [sb("w1_raw1_%d" % u, [P, PACK, H // 2], F32) for u in range(2)]
-        rest_sb = [sb("rest%d" % t, [P, S], F32) for t in range(PACK)]
-        wa_raw = sb("wa_raw", [P, PACK, N], F32)
-        wb_codes = sb("wb_codes", [P, N], U32)
-        read_sb = sb("read_sb", [P, N_TILES, PAIRS], F32)
-        gain_sb = sb("gain_sb", [P, PACK], F32)
-        low_sb = sb("low_sb", [P, PACK], F32)
+        def load(name, shape, source, on=None):
+            tile = sb(name, shape, F32, on=on)
+            nc.sync.dma_start(tile[:], source)
+            return tile
 
-        def table_words(a):
-            return tab_words[a].rearrange("p t i -> p (t i)").bitcast(I32)
+        def load_words(name, width, source, on=None):
+            tile = sb(name, [P, width], U32, on=on)
+            nc.sync.dma_start(tile[:].bitcast(I32), source.rearrange("p c i -> p (c i)").bitcast(I32))
+            return tile
 
         w1_rows = w1.rearrange("(a p j) r -> a p j r", a=PASSES, j=PACK)
         rest_rows = rest.rearrange("(p t) m -> p t m", t=PACK)
+        w2_raw = sb("w2_raw", [P, PASSES, 2 * H], U8)
         nc.sync.dma_start(offs_sb[:], offs)
         nc.sync.dma_start(tab_sc[LIVE:, :].bitcast(I32), tab_scales.rearrange("a q t -> q a t").bitcast(I32))
         nc.sync.dma_start(w2_sc_raw[LIVE:, :].bitcast(I32), w2_scales.rearrange("a q c -> q a c").bitcast(I32))
         nc.sync.dma_start(sc_rows[LIVE:, WB_AT:].bitcast(I32), wb_scales[0].rearrange("q (a c) -> (q a) c", a=2).bitcast(I32))
-        nc.sync.dma_start(w1_raw0[:], w1_rows[0])
-        nc.sync.dma_start(tab[0][:].bitcast(I32), table_words(0))
-        nc.sync.dma_start(w2_raw[:].bitcast(I32), w2_words.rearrange("a p b -> p a b").bitcast(I32))
-        nc.sync.dma_start(tab[1][:].bitcast(I32), table_words(1))
-        for u in range(2):
-            nc.sync.dma_start(w1_raw1[u][:], w1_rows[1][:, :, u * (H // 2) : (u + 1) * (H // 2)])
-        nc.sync.dma_start(rest_sb[0][:], rest_rows[:, 0, :])
-        nc.sync.dma_start(gain_sb[:], gain.rearrange("(p t) -> p t", t=PACK))
         nc.sync.dma_start(pos_sb[EARLY][:], pos1)
         nc.sync.dma_start(pos_sb[LATE][:], pos2)
-        nc.sync.dma_start(low_sb[:], low.rearrange("(p t) -> p t", t=PACK))
-        for t in range(1, PACK):
-            nc.sync.dma_start(rest_sb[t][:], rest_rows[:, t, :])
-        nc.sync.dma_start(wa_raw[:], wa.rearrange("(p j) n -> p j n", j=PACK))
-        nc.sync.dma_start(wb_codes[:].bitcast(I32), wb_words[0].rearrange("p c i -> p (c i)").bitcast(I32))
-        nc.sync.dma_start(read_sb[:], read.rearrange("(i p) j -> p i j", p=P))
+        nc.sync.dma_start(w2_raw[:].bitcast(I32), w2_words.rearrange("a p b -> p a b").bitcast(I32))
+        w1_raw0 = load("w1_raw0", [P, PACK, H], w1_rows[0])
+        tab = [load_words("tab0", T, tab_words[0])]
+        gain_sb = load("gain_sb", [P, PACK], gain.rearrange("(p t) -> p t", t=PACK))
+        low_sb = load("low_sb", [P, PACK], low.rearrange("(p t) -> p t", t=PACK))
 
         nc.vector.tensor_copy(
             sc_rows[:, W2_AT:WB_AT].rearrange("p (t m) -> p t m", t=PACK), w2_sc_raw[:].rearrange("p (m t) -> p t m", t=PACK)
@@ -104,9 +92,10 @@ def tile_list_motor_unit_readout_kernel(
         nc.vector.tensor_copy(v_sc_rows[:], tab_sc[:].indirect(offs_sb[:]))
         nc.vector.tensor_copy(sc_rows[LIVE:, V_AT:W2_AT].bitcast(I32), v_sc_rows[LIVE:, :].bitcast(I32))
         for q in range(4):
-            nc.gpsimd.dma_start(
+            nc.sync.dma_start(
                 planes[32 * q : 32 * q + 4, :, :].bitcast(I32), sc_rows[LIVE + 8 * q : LIVE + 8 * (q + 1), :].bitcast(I32)
             )
+        tab.append(load_words("tab1", T, tab_words[1], on="v_sc_rows"))
 
         v_codes = [[sb("v_codes%d_%d" % (a, h), [P, BANK], U32) for h in range(HALVES)] for a in range(PASSES)]
 
@@ -134,8 +123,14 @@ def tile_list_motor_unit_readout_kernel(
             )
 
         nc.scalar.copy(dealt(0, 0, P), by_line(w1_raw0))
+        w1_raw1 = [load("w1_raw1_0", [P, PACK, H // 2], w1_rows[1][:, :, : H // 2], on="w1_raw0")]
         quantise_w1(0, 0, PACK)
+        w1_raw1.append(load("w1_raw1_1", [P, PACK, H // 2], w1_rows[1][:, :, H // 2 :], on="w1_bf0"))
         gather_words(0)
+        rest_first = sb("rest_first", [P, 2, S], F32, on="tab0")
+        for t in range(2):
+            nc.sync.dma_start(rest_first[:, t, :], rest_rows[:, t, :])
+        rest_sb = [rest_first[:, t, :] for t in range(2)]
 
         w2_codes = sb("w2_codes", [P, PASSES, 2 * H], U8)
         nc.vector.tensor_copy(
@@ -144,13 +139,16 @@ def tile_list_motor_unit_readout_kernel(
         )
 
         gather_words(1)
+        rest_sb.append(load("rest2", [P, S], rest_rows[:, 2, :], on="v_sc_rows"))
         nc.scalar.copy(dealt(1, 0, P // 2), by_line(w1_raw1[0]))
         nc.vector.tensor_copy(dealt(1, P // 2, P), by_line(w1_raw1[1]))
+        rest_sb.append(load("rest3", [P, S], rest_rows[:, 3, :], on="w1_bf0"))
         quantise_w1(1, 0, 1)
         quantise_w1(1, 1, PACK)
+        wa_raw = load("wa_raw", [P, PACK, N], wa.rearrange("(p j) n -> p j n", j=PACK), on="w1_bf1")
 
         h_sb = [sb("h%d" % t, [P, S], F32) for t in range(PACK)]
-        cos_sb = [sb("cos%d" % t, [P, S], F32, on="w1_raw1_0" if t == 0 else None) for t in range(PACK)]
+        cos_sb = [sb("cos%d" % t, [P, S], F32, on="w1_raw0" if t == 0 else None) for t in range(PACK)]
         shape_ps = {}
 
         def table_product(acc, h, weights):
@@ -168,7 +166,7 @@ def tile_list_motor_unit_readout_kernel(
 
         def cosine(t):
             for h in range(HALVES):
-                phase = bank(4 + (HALVES * t + h) % 4, [P, BANK], "phase")
+                phase = bank((4 + HALVES * t if t < 2 else 0) + h, [P, BANK], "phase")
                 table_product(
                     phase,
                     h,
@@ -183,7 +181,7 @@ def tile_list_motor_unit_readout_kernel(
         def shape_product(t):
             rows = slice(t * P, (t + 1) * P)
             for h in range(HALVES):
-                shape_ps[t, h] = bank((HALVES * t + h) % 4, [P, BANK], "shape_ps")
+                shape_ps[t, h] = bank(HALVES * min(t, 1) + h, [P, BANK], "shape_ps")
                 table_product(shape_ps[t, h], h, lambda a: (w1_codes[a][:, rows].bitcast(FP8X4), w1_sc[a][:, rows]))
 
         def add_rest(t, h):
@@ -222,17 +220,21 @@ def tile_list_motor_unit_readout_kernel(
         for t in range(PACK):
             if t + 2 < PACK:
                 cosine(t + 2)
-                shape_product(t + 2)
             if t + 1 < PACK:
                 add_rest(t + 1, 0)
             nc.vector.scalar_tensor_tensor(h_sb[t][:], h_sb[t][:], gain_sb[:, t : t + 1], cos_sb[t][:], ALU.mult, ALU.mult)
             if t + 1 < PACK:
                 add_rest(t + 1, 1)
+            if t + 2 < PACK:
+                shape_product(t + 2)
+            if t == 0:
+                wb_codes = load_words("wb_codes", N, wb_words[0], on="w1_raw0")
+                read_sb = load("read_sb", [P, N_TILES, PAIRS], read.rearrange("(i p) j -> p i j", p=P), on="tab0")
             pick(0, LATE, t)
             pick(0, EARLY, t)
             bound_below(0, t)
 
-        wa_bf = sb("wa_bf", [P, N, PACK], BF16, on="rest%d" % (PACK - 1))
+        wa_bf = sb("wa_bf", [P, N, PACK], BF16, on="w1_bf0")
         for u in range(2):
             quantise_wa(wa_bf, u)
 

@@ -166,7 +166,7 @@ def tile_list_motor_unit_readout_kernel(
 
         def cosine(t):
             for h in range(HALVES):
-                phase = bank((4 + HALVES * t if t < 2 else 0) + h, [P, BANK], "phase")
+                phase = bank((4 + HALVES * t + h) % 8, [P, BANK], "phase")
                 table_product(
                     phase,
                     h,
@@ -181,21 +181,14 @@ def tile_list_motor_unit_readout_kernel(
         def shape_product(t):
             rows = slice(t * P, (t + 1) * P)
             for h in range(HALVES):
-                shape_ps[t, h] = bank(HALVES * min(t, 1) + h, [P, BANK], "shape_ps")
+                shape_ps[t, h] = bank(HALVES * t + h, [P, BANK], "shape_ps")
                 table_product(shape_ps[t, h], h, lambda a: (w1_codes[a][:, rows].bitcast(FP8X4), w1_sc[a][:, rows]))
 
         def add_rest(t, h):
             cols = slice(h * BANK, (h + 1) * BANK)
             nc.vector.tensor_tensor(h_sb[t][:, cols], shape_ps[t, h][:], rest_sb[t][:, cols], ALU.add)
 
-        picked = {}
-
-        def pick(g, i, t):
-            cols = slice(g * WIDTH // LIST_ROWS, (g + 1) * WIDTH // LIST_ROWS)
-            nc.vector.tensor_copy(picked[g, i][:, t, :], h_sb[t][:].indirect(pos_sb[i][:, cols]))
-
-        def bound_below(g, t):
-            nc.vector.tensor_scalar(picked[g, LATE][:, t, :], picked[g, LATE][:, t, :], low_sb[:, t : t + 1], None, ALU.max)
+        picked = [sb("picked%d" % i, [P, PACK, PAIRS], F32) for i in (EARLY, LATE)]
 
         wa_codes = sb("wa_codes", [P, N], U32)
         wa_sc = sb("wa_sc", [P, N], U8)
@@ -209,30 +202,35 @@ def tile_list_motor_unit_readout_kernel(
                 out=wa_codes[:, cols].bitcast(FP8X4), scales=wa_sc[:, cols], in_=wa_bf[:, cols, :].rearrange("p c j -> p (c j)")
             )
 
-        for i in (EARLY, LATE):
-            picked[0, i] = sb("picked0_%d" % i, [P, PACK, WIDTH], F32)
         for t in range(2):
             cosine(t)
-        for t in range(2):
-            shape_product(t)
-        for h in range(HALVES):
-            add_rest(0, h)
         for t in range(PACK):
-            if t + 2 < PACK:
-                cosine(t + 2)
-            if t + 1 < PACK:
-                add_rest(t + 1, 0)
-            nc.vector.scalar_tensor_tensor(h_sb[t][:], h_sb[t][:], gain_sb[:, t : t + 1], cos_sb[t][:], ALU.mult, ALU.mult)
-            if t + 1 < PACK:
-                add_rest(t + 1, 1)
-            if t + 2 < PACK:
-                shape_product(t + 2)
+            shape_product(t)
+        for t in range(2):
+            for h in range(HALVES):
+                add_rest(t, h)
+        for t in range(2, PACK):
+            cosine(t)
+        for t in range(2, PACK):
+            for h in range(HALVES):
+                add_rest(t, h)
+        for t in range(PACK):
+            nc.gpsimd.tensor_tensor(h_sb[t][:], h_sb[t][:], cos_sb[t][:], ALU.mult)
             if t == 0:
                 wb_codes = load_words("wb_codes", N, wb_words[0], on="w1_raw0")
                 read_sb = load("read_sb", [P, N_TILES, PAIRS], read.rearrange("(i p) j -> p i j", p=P), on="tab0")
-            pick(0, LATE, t)
-            pick(0, EARLY, t)
-            bound_below(0, t)
+            early, late = picked[EARLY][:, t, :], picked[LATE][:, t, :]
+            nc.vector.tensor_copy(late, h_sb[t][:].indirect(pos_sb[LATE][:]))
+            if t == PACK - 1:
+                bounded = sb("bounded", [P, PACK, PAIRS], F32, on="cos%d" % t)
+                for u in range(PACK):
+                    nc.vector.tensor_scalar(
+                        bounded[:, u, :], picked[LATE][:, u, :], gain_sb[:, u : u + 1], low_sb[:, u : u + 1], ALU.mult, ALU.max
+                    )
+            nc.vector.tensor_copy(early, h_sb[t][:].indirect(pos_sb[EARLY][:]))
+            nc.scalar.activation(early, early, ACT.Abs, scale=gain_sb[:, t : t + 1])
+
+        x_rows = [picked[EARLY], bounded]
 
         wa_bf = sb("wa_bf", [P, N, PACK], BF16, on="w1_bf0")
         for u in range(2):
@@ -249,9 +247,9 @@ def tile_list_motor_unit_readout_kernel(
             x_codes[g, i] = sb("x_codes%d_%d" % (g, i), [P, WIDTH], U32)
             x_sc[g, i] = sb("x_sc%d_%d" % (g, i), [P, WIDTH], U8)
             woven = x_bf[:].rearrange("p (c e) t -> p c t e", e=4)
-            source = picked[g, i][:].rearrange("p t (c e) -> p c t e", e=4)
+            source = x_rows[i][:, :, g * WIDTH : (g + 1) * WIDTH].rearrange("p t (c e) -> p c t e", e=4)
             if i == EARLY:
-                nc.scalar.activation(woven, source, ACT.Abs)
+                nc.vector.tensor_copy(woven, source)
             else:
                 nc.scalar.copy(woven, source)
             nc.vector.quantize_mx(
@@ -279,15 +277,8 @@ def tile_list_motor_unit_readout_kernel(
 
         for g in range(PARTS):
             ys = [bank(index, [P, per_bank, WIDTH], "y") for index in y_banks[g]]
-            order = (LATE, EARLY) if g == 0 else (EARLY, LATE)
+            order = (LATE, EARLY)
             for i in order:
-                if g > 0:
-                    picked[g, i] = sb("picked1_%d" % i, [P, PACK, WIDTH], F32, on="cos3" if i == EARLY else "x_bf0_0")
-                    for t in range(PACK):
-                        pick(g, i, t)
-                    if i == LATE:
-                        for t in range(PACK):
-                            bound_below(g, t)
                 quantise_x(g, i)
                 if i == order[0]:
                     for b, y in enumerate(ys):

import math
from contextlib import ExitStack

import concourse.mybir as mybir

K, T, S, H, PAIRS, N = 1024, 4096, 1024, 512, 512, 768
FLOPS = 2 * (2 * K * H * S + 2 * H * N * PAIRS)

F32 = mybir.dt.float32
BF16 = mybir.dt.bfloat16
I32 = mybir.dt.int32
U32 = mybir.dt.uint32
U16 = mybir.dt.uint16
U8 = mybir.dt.uint8
FP8X4 = mybir.dt.float8_e4m3fn_x4
FP4X4 = mybir.dt.float4_e2m1fn_x4
ALU = mybir.AluOpType
ACT = mybir.ActivationFunctionType

P = 128
PACK = 4
PASSES = K // (P * PACK)
BANK = 512
HALVES = S // BANK
N_TILES = N // P
LIST_ROWS = 16
LIVE = 96
PARTS = 2
WIDTH = PAIRS // PARTS
V_AT, W2_AT, WB_AT, SC_WIDTH = 0, S, S + H, S + H + N // 2
EARLY, LATE = 0, 1


def tile_list_motor_unit_readout_kernel(
    tc, tab_words, tab_scales, offs, pos1, pos2, w1, w2_words, w2_scales, rest, gain, low, wa, wb_words, wb_scales, read, out
):
    nc = tc.nc
    with ExitStack() as ctx:
        keep = ctx.enter_context(tc.tile_pool(name="keep", bufs=1))
        psum = ctx.enter_context(tc.psum_pool(name="psum", bufs=1))

        def sb(name, shape, dtype, on=None):
            return keep.tile(shape, dtype, name=name, tag=on or name, align_bytes=64)

        def bank(index, shape, name):
            return psum.tile(shape, F32, name=name, tag="bank%d" % index)

        offs_sb = keep.tile([P, S // LIST_ROWS], U16, name="offs_sb")
        pos_sb = [keep.tile([P, PAIRS // LIST_ROWS], U16, name="pos_sb%d" % i) for i in range(2)]

        tab_sc = sb("tab_sc", [P, T], U8)
        w2_sc_raw = sb("w2_sc_raw", [P, H], U8)
        sc_rows = sb("sc_rows", [P, SC_WIDTH], U8)
        planes = sb("planes", [P, PASSES, SC_WIDTH], U8)
        nc.vector.memset(w2_sc_raw[:LIVE, :].bitcast(I32), 0)
        nc.vector.memset(tab_sc[:LIVE, :].bitcast(I32), 0)
        nc.vector.memset(planes[:].bitcast(I32), 0)

        warm = sb("warm", [P, 1], F32)
        nc.vector.memset(warm[:], 0.0)
        nc.scalar.activation(warm[:], warm[:], ACT.Sin)

        def load(name, shape, source, on=None):
            tile = sb(name, shape, F32, on=on)
            nc.sync.dma_start(tile[:], source)
            return tile

        def load_words(name, width, source, on=None):
            tile = sb(name, [P, width], U32, on=on)
            nc.sync.dma_start(tile[:].bitcast(I32), source.rearrange("p c i -> p (c i)").bitcast(I32))
            return tile

        w1_rows = w1.rearrange("(a p j) r -> a p j r", a=PASSES, j=PACK)
        rest_rows = rest.rearrange("(p t) m -> p t m", t=PACK)
        w2_raw = sb("w2_raw", [P, PASSES, 2 * H], U8)
        nc.sync.dma_start(offs_sb[:], offs)
        nc.sync.dma_start(tab_sc[LIVE:, :].bitcast(I32), tab_scales.rearrange("a q t -> q a t").bitcast(I32))
        nc.sync.dma_start(w2_sc_raw[LIVE:, :].bitcast(I32), w2_scales.rearrange("a q c -> q a c").bitcast(I32))
        nc.sync.dma_start(sc_rows[LIVE:, WB_AT:].bitcast(I32), wb_scales[0].rearrange("q (a c) -> (q a) c", a=2).bitcast(I32))
        nc.sync.dma_start(pos_sb[EARLY][:], pos1)
        nc.sync.dma_start(pos_sb[LATE][:], pos2)
        nc.sync.dma_start(w2_raw[:].bitcast(I32), w2_words.rearrange("a p b -> p a b").bitcast(I32))
        w1_raw0 = load("w1_raw0", [P, PACK, H], w1_rows[0])
        tab = [load_words("tab0", T, tab_words[0])]
        gain_sb = load("gain_sb", [P, PACK], gain.rearrange("(p t) -> p t", t=PACK))
        low_sb = load("low_sb", [P, PACK], low.rearrange("(p t) -> p t", t=PACK))

        nc.vector.tensor_copy(
            sc_rows[:, W2_AT:WB_AT].rearrange("p (t m) -> p t m", t=PACK), w2_sc_raw[:].rearrange("p (m t) -> p t m", t=PACK)
        )
        v_sc_rows = sb("v_sc_rows", [P, S], U8)
        nc.vector.tensor_copy(v_sc_rows[:], tab_sc[:].indirect(offs_sb[:]))
        nc.vector.tensor_copy(sc_rows[LIVE:, V_AT:W2_AT].bitcast(I32), v_sc_rows[LIVE:, :].bitcast(I32))
        for q in range(4):
            nc.sync.dma_start(
                planes[32 * q : 32 * q + 4, :, :].bitcast(I32), sc_rows[LIVE + 8 * q : LIVE + 8 * (q + 1), :].bitcast(I32)
            )
        tab.append(load_words("tab1", T, tab_words[1], on="v_sc_rows"))

        v_codes = [[sb("v_codes%d_%d" % (a, h), [P, BANK], U32) for h in range(HALVES)] for a in range(PASSES)]

        def gather_words(a):
            cols = BANK // LIST_ROWS
            for h in range(HALVES):
                nc.vector.tensor_copy(v_codes[a][h][:], tab[a][:].indirect(offs_sb[:, h * cols : (h + 1) * cols]))

        w1_bf = [sb("w1_bf%d" % a, [P, PACK, P, PACK], BF16) for a in range(PASSES)]
        w1_codes = [sb("w1_codes%d" % a, [P, H], U32) for a in range(PASSES)]
        w1_sc = [sb("w1_sc%d" % a, [P, H], U8) for a in range(PASSES)]

        def dealt(a, m0, m1):
            return w1_bf[a][:, :, m0:m1, :].rearrange("p t m j -> p m t j")

        def by_line(raw):
            return raw[:].rearrange("p j (m t) -> p m t j", t=PACK)

        def quantise_w1(a, t0, t1):
            cols = slice(t0 * P, t1 * P)
            nc.vector.quantize_mx(
                out=w1_codes[a][:, cols].bitcast(FP8X4),
                scales=w1_sc[a][:, cols],
                in_=w1_bf[a][:, t0:t1, :, :].rearrange("p t m j -> p (t m j)"),
            )

        nc.scalar.copy(dealt(0, 0, P), by_line(w1_raw0))
        w1_raw1 = [load("w1_raw1_0", [P, PACK, H // 2], w1_rows[1][:, :, : H // 2], on="w1_raw0")]
        quantise_w1(0, 0, PACK)
        w1_raw1.append(load("w1_raw1_1", [P, PACK, H // 2], w1_rows[1][:, :, H // 2 :], on="w1_bf0"))
        gather_words(0)
        rest_first = sb("rest_first", [P, 2, S], F32, on="tab0")
        for t in range(2):
            nc.sync.dma_start(rest_first[:, t, :], rest_rows[:, t, :])
        rest_sb = [rest_first[:, t, :] for t in range(2)]

        w2_codes = sb("w2_codes", [P, PASSES, 2 * H], U8)
        nc.vector.tensor_copy(
            w2_codes[:].bitcast(U16).rearrange("p a (t m) -> p a t m", t=PACK),
            w2_raw[:].bitcast(U16).rearrange("p a (m t) -> p a t m", t=PACK),
        )

        gather_words(1)
        rest_sb.append(load("rest2", [P, S], rest_rows[:, 2, :], on="v_sc_rows"))
        nc.scalar.copy(dealt(1, 0, P // 2), by_line(w1_raw1[0]))
        nc.vector.tensor_copy(dealt(1, P // 2, P), by_line(w1_raw1[1]))
        rest_sb.append(load("rest3", [P, S], rest_rows[:, 3, :], on="w1_bf0"))
        quantise_w1(1, 0, 1)
        quantise_w1(1, 1, PACK)
        wa_raw = load("wa_raw", [P, PACK, N], wa.rearrange("(p j) n -> p j n", j=PACK), on="w1_bf1")

        h_sb = [sb("h%d" % t, [P, S], F32) for t in range(PACK)]
        cos_sb = [sb("cos%d" % t, [P, S], F32, on="w1_raw0" if t == 0 else None) for t in range(PACK)]
        shape_ps = {}

        def table_product(acc, h, weights):
            for a in range(PASSES):
                codes, scales = weights(a)
                nc.tensor.matmul_mx(
                    out=acc[:],
                    lhsT=codes,
                    lhsT_scale=scales,
                    rhs=v_codes[a][h][:].bitcast(FP8X4),
                    rhs_scale=planes[:, a, V_AT + h * BANK : V_AT + (h + 1) * BANK],
                    start=(a == 0),
                    stop=(a == PASSES - 1),
                )

        def cosine(t):
            for h in range(HALVES):
                phase = bank((4 + HALVES * t + h) % 8, [P, BANK], "phase")
                table_product(
                    phase,
                    h,
                    lambda a: (
                        w2_codes[:, a, 2 * t * P : 2 * (t + 1) * P].bitcast(FP4X4),
                        planes[:, a, W2_AT + t * P : W2_AT + (t + 1) * P],
                    ),
                )
                nc.scalar.activation(cos_sb[t][:, h * BANK : (h + 1) * BANK], phase[:], ACT.Abs)
            nc.scalar.activation(cos_sb[t][:], cos_sb[t][:], ACT.Sin, bias=math.pi / 2, scale=-1.0)

        def shape_product(t):
            rows = slice(t * P, (t + 1) * P)
            for h in range(HALVES):
                shape_ps[t, h] = bank(HALVES * t + h, [P, BANK], "shape_ps")
                table_product(shape_ps[t, h], h, lambda a: (w1_codes[a][:, rows].bitcast(FP8X4), w1_sc[a][:, rows]))

        def add_rest(t, h):
            cols = slice(h * BANK, (h + 1) * BANK)
            nc.vector.tensor_tensor(h_sb[t][:, cols], shape_ps[t, h][:], rest_sb[t][:, cols], ALU.add)

        picked = [sb("picked%d" % i, [P, PACK, PAIRS], F32) for i in (EARLY, LATE)]

        wa_codes = sb("wa_codes", [P, N], U32)
        wa_sc = sb("wa_sc", [P, N], U8)

        def quantise_wa(wa_bf, u):
            cols = slice(u * (N // 2), (u + 1) * (N // 2))
            nc.scalar.copy(
                wa_bf[:, cols, :].rearrange("p (c i) j -> p c j i", i=4), wa_raw[:, :, cols].rearrange("p j (c i) -> p c j i", i=4)
            )
            nc.vector.quantize_mx(
                out=wa_codes[:, cols].bitcast(FP8X4), scales=wa_sc[:, cols], in_=wa_bf[:, cols, :].rearrange("p c j -> p (c j)")
            )

        for t in range(2):
            cosine(t)
        for t in range(PACK):
            shape_product(t)
        for t in range(2):
            for h in range(HALVES):
                add_rest(t, h)
        for t in range(2, PACK):
            cosine(t)
        for t in range(2, PACK):
            for h in range(HALVES):
                add_rest(t, h)
        for t in range(PACK):
            nc.gpsimd.tensor_tensor(h_sb[t][:], h_sb[t][:], cos_sb[t][:], ALU.mult)
            if t == 0:
                wb_codes = load_words("wb_codes", N, wb_words[0], on="w1_raw0")
                read_sb = load("read_sb", [P, N_TILES, PAIRS], read.rearrange("(i p) j -> p i j", p=P), on="tab0")
            early, late = picked[EARLY][:, t, :], picked[LATE][:, t, :]
            nc.vector.tensor_copy(late, h_sb[t][:].indirect(pos_sb[LATE][:]))
            if t == PACK - 1:
                bounded = sb("bounded", [P, PACK, PAIRS], F32, on="cos%d" % t)
                for u in range(PACK):
                    nc.vector.tensor_scalar(
                        bounded[:, u, :], picked[LATE][:, u, :], gain_sb[:, u : u + 1], low_sb[:, u : u + 1], ALU.mult, ALU.max
                    )
            nc.vector.tensor_copy(early, h_sb[t][:].indirect(pos_sb[EARLY][:]))
            nc.scalar.activation(early, early, ACT.Abs, scale=gain_sb[:, t : t + 1])

        x_rows = [picked[EARLY], bounded]

        wa_bf = sb("wa_bf", [P, N, PACK], BF16, on="w1_bf0")
        for u in range(2):
            quantise_wa(wa_bf, u)

        out_rows = out.rearrange("(i p) j -> p i j", p=P)
        y_banks = ((4, 5, 6), (7, 0, 1))
        per_bank = BANK // WIDTH

        x_codes, x_sc = {}, {}

        def quantise_x(g, i):
            x_bf = sb("x_bf%d_%d" % (g, i), [P, WIDTH, PACK], BF16)
            x_codes[g, i] = sb("x_codes%d_%d" % (g, i), [P, WIDTH], U32)
            x_sc[g, i] = sb("x_sc%d_%d" % (g, i), [P, WIDTH], U8)
            woven = x_bf[:].rearrange("p (c e) t -> p c t e", e=4)
            source = x_rows[i][:, :, g * WIDTH : (g + 1) * WIDTH].rearrange("p t (c e) -> p c t e", e=4)
            if i == EARLY:
                nc.vector.tensor_copy(woven, source)
            else:
                nc.scalar.copy(woven, source)
            nc.vector.quantize_mx(
                out=x_codes[g, i][:].bitcast(FP8X4), scales=x_sc[g, i][:], in_=x_bf[:].rearrange("p w t -> p (w t)")
            )

        def product(g, i, y, b, first):
            for e in range(per_bank):
                n_tile = b * per_bank + e
                cols = slice(n_tile * P, (n_tile + 1) * P)
                if i == EARLY:
                    codes, scales = wa_codes[:, cols], wa_sc[:, cols]
                else:
                    wb_at = WB_AT + (n_tile % (N_TILES // 2)) * P
                    codes, scales = wb_codes[:, cols], planes[:, n_tile // (N_TILES // 2), wb_at : wb_at + P]
                nc.tensor.matmul_mx(
                    out=y[:, e, :],
                    lhsT=codes.bitcast(FP8X4),
                    lhsT_scale=scales,
                    rhs=x_codes[g, i][:].bitcast(FP8X4),
                    rhs_scale=x_sc[g, i][:],
                    start=(first and e == 0),
                    stop=(not first and e == per_bank - 1),
                )

        for g in range(PARTS):
            ys = [bank(index, [P, per_bank, WIDTH], "y") for index in y_banks[g]]
            order = (LATE, EARLY)
            for i in order:
                quantise_x(g, i)
                if i == order[0]:
                    for b, y in enumerate(ys):
                        product(g, i, y, b, True)
            pairs = slice(g * WIDTH, (g + 1) * WIDTH)
            for b, y in enumerate(ys):
                tiles = slice(b * per_bank, (b + 1) * per_bank)
                product(g, order[1], y, b, False)
                result = sb("result%d_%d" % (g, b), [P, per_bank, WIDTH], F32)
                nc.vector.tensor_tensor(result[:], y[:], read_sb[:, tiles, pairs], ALU.mult)
                nc.sync.dma_start(out_rows[:, tiles, pairs], result[:])
